import numpy as np
import ml_dtypes


def mxq(x, axis, fmt="e4m3"):
    dtype, down = {"e4m3": (ml_dtypes.float8_e4m3fn, 7), "e5m2": (ml_dtypes.float8_e5m2, 14)}[fmt]
    v = np.moveaxis(np.asarray(x, np.float32).astype(ml_dtypes.bfloat16).astype(np.float64), axis, -1)
    blocks = v.reshape(v.shape[:-1] + (-1, 32))
    amax = np.abs(blocks).max(-1, keepdims=True)
    byte = np.maximum(np.where(amax > 0, np.frexp(amax)[1] - 1 + 127, 0) - down, 1)
    scale = np.exp2(byte - 127.0)
    codes = (blocks / scale).astype(np.float32).astype(dtype).astype(np.float64)
    return np.moveaxis((codes * scale).reshape(v.shape), -1, axis)


WIDE = False


def mx_kscale(k):
    if not WIDE:
        return np.ones(k)
    levels = np.array([10, -10, 5, -5, 0])
    if k % 512:
        return np.exp2(np.random.permutation(np.resize(levels, k // 32))).repeat(32)
    a = np.empty((k // 512, 16))
    for p in range(k // 512):
        a[p, :8] = np.random.permutation(np.resize(levels, 8))
        for g in range(8):
            far = levels[np.abs(levels - a[p, g]) >= 10]
            a[p, g + 8] = far[np.random.randint(len(far))]
    return np.exp2(a.ravel()).repeat(32)


def f64(x):
    return np.asarray(x).astype(np.float64)


def striped(idx):
    return np.tile(idx.reshape(-1, 16).T, (8, 1)).astype(np.uint16)


def unstriped(offs):
    return offs[:16].T.reshape(-1).astype(np.int64)


def pack_weight(w):
    k, n = w.shape
    w = f64(np.asarray(w, np.float32).astype(ml_dtypes.bfloat16)).reshape(k // 32, 32, n)
    amax = np.abs(w).max(1)
    byte = np.clip(np.where(amax > 0, np.frexp(amax)[1] - 1 + 127 - 7, 1), 1, 254)
    scaled = (w * np.exp2(127.0 - byte)[:, None, :]).reshape(k, n).astype(np.float32)
    words = np.ascontiguousarray(scaled.reshape(k // 512, 128, 4, n).transpose(0, 1, 3, 2)).astype(ml_dtypes.float8_e4m3fn).view(np.uint8)
    return words, np.ascontiguousarray(byte.astype(np.uint8).reshape(k // 512, 16, n))


def unpack_weight(words, scales):
    g, p, n, _ = words.shape
    vals = np.ascontiguousarray(words).view(ml_dtypes.float8_e4m3fn).astype(np.float64) * np.repeat(np.exp2(scales.astype(np.float64) - 127.0), 8, axis=1)[..., None]
    return vals.transpose(0, 1, 3, 2).reshape(g * 512, n)


def sigmoid(v):
    return 1.0 / (1.0 + np.exp(-np.maximum(v, -700.0)))


K, T, S, N, H, J = 512, 2048, 512, 512, 512, 512


def setup_inputs():
    n = np.random.standard_normal
    s = mx_kscale(K)[:, None]
    u = mx_kscale(S)
    packed_xT = pack_weight(n((K, T)) * s)
    return {
        "x_words": packed_xT[0],
        "x_scales": packed_xT[1],
        "wa": (n((K, H)) / np.sqrt(K) / s).astype(np.float32),
        "wb": (n((K, H)) / np.sqrt(K) / s).astype(np.float32),
        "gt": (np.random.uniform(0.5, 1.5, (S, 1)) * u[:, None]).astype(np.float32),
        "w1": (n((S, N)) / np.sqrt(S) / u[:, None]).astype(np.float32),
        "tab": n((N, J)).astype(np.float32),
        "offs": striped(np.random.permutation(T)[:S]),
        "two": striped(np.random.permutation(T)[:S]),
        "n1": striped(np.random.permutation(H)),
        "n2": striped(np.random.permutation(H)),
        "n3": striped(np.random.randint(0, J, H)),
        "n4": striped(np.random.randint(0, J, H)),
        "n5": striped(np.random.permutation(H)),
    }


def reference(x_words, x_scales, wa, wb, gt, w1, tab, offs, two, n1, n2, n3, n4, n5):
    xq = unpack_weight(x_words, x_scales)[:, unstriped(offs)]
    y = xq.T @ mxq(f64(wa), 0, "e4m3")
    x_two = unpack_weight(x_words, x_scales)[:, unstriped(two)]
    d = x_two.T @ mxq(f64(wb), 0, "e4m3")
    z = f64(gt) * ((y + y[:, unstriped(n1)]) * (sigmoid(d + d[:, unstriped(n2)])))
    h = mxq(f64(w1), 0, "e4m3").T @ mxq(z, 0, "e4m3")
    return h[:, unstriped(n5)] * f64(tab)[:, unstriped(n3)] + f64(tab)[:, unstriped(n4)]

@@ -1,0 +1,264 @@
+from contextlib import ExitStack
+
+import concourse.mybir as mybir
+from concourse.masks import make_identity
+
+K, T, S, N, H, J = 512, 2048, 512, 512, 512, 512
+FLOPS = 2 * S * K * H * 2 + 2 * N * S * H
+
+F32 = mybir.dt.float32
+BF16 = mybir.dt.bfloat16
+I32 = mybir.dt.int32
+U32 = mybir.dt.uint32
+U16 = mybir.dt.uint16
+U8 = mybir.dt.uint8
+FP8X4 = mybir.dt.float8_e4m3fn_x4
+ACT = mybir.ActivationFunctionType
+ALU = mybir.AluOpType
+
+P = 128
+PACK = 4
+TILES = 4
+HALF = 256
+LIST_ROWS = 16
+YCOPY = "ssss"
+DCOPY = "vvvv"
+N2 = ["vvvv","vvss"]
+N3 = "vvvs"
+ZCOPY = "vv"
+HCOPY = ["ssss","vvvv"]
+CAST = {"wa":"v","wb":"s","w1":"v"}
+SPLIT = [256,256]
+LATE = [2,3]
+TAGS = {"wb_codes":"x_codes","tab4_3":"d3","tab3_2":"wb_bf16","tab3_3":"yg","h0":"y0","h1":"y1","h2":"y2","h3":"y3"}
+HOLD = 0
+
+
+def tile_picked_twttriebkinda_none_p_kernel(tc, x_words, x_scales, wa, wb, gt, w1, tab, offs, two, n1, n2, n3, n4, n5, out):
+    nc = tc.nc
+    with ExitStack() as ctx:
+        keep = ctx.enter_context(tc.tile_pool(name="keep", bufs=1))
+        ring = ctx.enter_context(tc.tile_pool(name="ring", bufs=2))
+        psum = ctx.enter_context(tc.psum_pool(name="psum", bufs=1))
+
+        def load_list(name, src):
+            tile = keep.tile([P, S // LIST_ROWS], U16, name=name)
+            nc.sync.dma_start(tile[:], src)
+            return tile
+
+        def load_weight(name, src):
+            raw = keep.tile([P, PACK, 512], F32, name=name)
+            nc.sync.dma_start(out=raw[:], in_=src.rearrange("(p j) n -> p j n", j=PACK))
+            return raw
+
+        def load_tab(mt):
+            tile = keep.tile([P, J], F32, name="tab%d" % mt)
+            nc.sync.dma_start(out=tile[:], in_=tab[mt * P : (mt + 1) * P, :])
+            return tile
+
+        def part(lst, c0, c1):
+            return lst[:, c0 // LIST_ROWS : c1 // LIST_ROWS]
+
+        def gather(eng, dst, window, lst):
+            if eng == "s":
+                nc.scalar.activation(dst, window[:].indirect(lst), ACT.Copy)
+            else:
+                nc.vector.tensor_copy(dst, window[:].indirect(lst))
+
+        def copy(eng, dst, src):
+            if eng == "s":
+                nc.scalar.copy(dst, src)
+            elif eng == "v":
+                nc.vector.tensor_copy(dst, src)
+            else:
+                nc.gpsimd.tensor_copy(dst, src)
+
+        x_bytes = keep.tile([P, T], U8, name="x_bytes", align_bytes=64)
+        nc.vector.memset(x_bytes[:].bitcast(I32), 0)
+        x_codes = keep.tile([P, T], U32, name="x_codes", align_bytes=64)
+        gt_cols = keep.tile([P, TILES], F32, name="gt_cols")
+        tabs = [None] * TILES
+        l4 = load_list("l4", n4)
+        tabs[0] = load_tab(0)
+        l3 = load_list("l3", n3)
+        tabs[1] = load_tab(1)
+        l_offs = load_list("l_offs", offs)
+        l_two = load_list("l_two", two)
+        wa_raw = load_weight("wa_raw", wa)
+        for q in range(4):
+            nc.sync.dma_start(
+                out=x_bytes[32 * q : 32 * q + 4, :].bitcast(I32),
+                in_=x_scales[0, 4 * q : 4 * q + 4, :].bitcast(I32),
+            )
+        wb_raw = load_weight("wb_raw", wb)
+        nc.sync.dma_start(out=x_codes[:].bitcast(I32), in_=x_words[0].rearrange("p n t -> p (n t)").bitcast(I32))
+        tabs[2] = load_tab(2)
+        l1 = load_list("l1", n1)
+        l2 = load_list("l2", n2)
+        w1_raw = load_weight("w1_raw", w1)
+        tabs[3] = load_tab(3)
+        l5 = load_list("l5", n5)
+        with nc.allow_non_contiguous_dma(reason="one weight a row"):
+            nc.scalar.dma_start(out=gt_cols[:], in_=gt.rearrange("(t p) o -> p (t o)", p=P))
+
+        ident = keep.tile([P, P], F32, name="ident")
+        make_identity(nc, ident[:])
+        half_gt = keep.tile([P, TILES], F32, name="half_gt")
+        nc.vector.tensor_scalar(half_gt[:], gt_cols[:], 0.5, None, ALU.mult)
+
+        tab3, tab4 = {}, {}
+
+        def fetch(key, store, eng, lst, mt):
+            name = "tab%s_%d" % (key, mt)
+            tile = keep.tile([P, H], F32, name=name, tag=TAGS.get(name, name), align_bytes=64)
+            for hb in range(2):
+                gather(eng, tile[:, hb * HALF : (hb + 1) * HALF], tabs[mt], part(lst, hb * HALF, (hb + 1) * HALF))
+            store[mt] = tile
+
+        for mt in range(2):
+            fetch("4", tab4, "s", l4, mt)
+            fetch("3", tab3, N3[mt], l3, mt)
+
+        def pick(name, dtype, window, lst):
+            picked = keep.tile([P, S], dtype, name=name, align_bytes=64)
+            nc.vector.tensor_copy(picked[:], window[:].indirect(lst[:]))
+            return picked
+
+        def quantise_weight(name, raw):
+            grouped = keep.tile([P, 512, PACK], BF16, name=name + "_bf16", tag=TAGS.get(name + "_bf16", name + "_bf16"), align_bytes=64)
+            engs = CAST[name]
+            width = 512 // len(engs)
+            for k, eng in enumerate(engs):
+                copy(
+                    eng,
+                    grouped[:, k * width : (k + 1) * width, :].rearrange("p (c i) j -> p c j i", i=4),
+                    raw[:, :, k * width : (k + 1) * width].rearrange("p j (c i) -> p c j i", i=4),
+                )
+            codes = keep.tile([P, 512], U32, name=name + "_codes", tag=TAGS.get(name + "_codes", name + "_codes"), align_bytes=64)
+            scales = keep.tile([P, 512], U8, name=name + "_scales", align_bytes=64)
+            nc.vector.quantize_mx(out=codes[:].bitcast(FP8X4), scales=scales[:], in_=grouped[:].rearrange("p c j -> p (c j)"))
+            return codes, scales
+
+        def mx(acc, lhs, lhs_cols, rhs, rhs_cols):
+            nc.tensor.matmul_mx(
+                out=acc,
+                lhsT=lhs[0][:, lhs_cols].bitcast(FP8X4),
+                lhsT_scale=lhs[1][:, lhs_cols],
+                rhs=rhs[0][:, rhs_cols].bitcast(FP8X4),
+                rhs_scale=rhs[1][:, rhs_cols],
+                start=True,
+                stop=True,
+            )
+
+        ys, ds = [], []
+
+        def project_y(x_offs, wa_q):
+            for t in range(TILES):
+                bank = psum.tile([P, H], F32, name="ymm", tag="bank%d" % t)
+                mx(bank[:], x_offs, slice(t * P, (t + 1) * P), wa_q, slice(0, H))
+                y = keep.tile([P, H], F32, name="y%d" % t, align_bytes=64)
+                if YCOPY[t] == "s":
+                    nc.scalar.activation(y[:], bank[:], ACT.Copy, scale=half_gt[:, t : t + 1])
+                else:
+                    nc.vector.tensor_scalar(y[:], bank[:], half_gt[:, t : t + 1], None, ALU.mult)
+                ys.append(y)
+
+        def project_d(x_two, wb_q):
+            for t in range(TILES):
+                bank = psum.tile([P, H], F32, name="dmm", tag="bank%d" % (4 + t))
+                mx(bank[:], x_two, slice(t * P, (t + 1) * P), wb_q, slice(0, H))
+                d = keep.tile([P, H], F32, name="d%d" % t, align_bytes=64)
+                copy(DCOPY[t], d[:], bank[:])
+                ds.append(d)
+
+        offs_scales = pick("offs_scales", U8, x_bytes, l_offs)
+        two_scales = pick("two_scales", U8, x_bytes, l_two)
+        wa_q = quantise_weight("wa", wa_raw)
+        offs_codes = pick("offs_codes", U32, x_codes, l_offs)
+        two_codes = pick("two_codes", U32, x_codes, l_two)
+        wb_q = quantise_weight("wb", wb_raw)
+        project_y((offs_codes, offs_scales), wa_q)
+        project_d((two_codes, two_scales), wb_q)
+
+        def turned_sum(tag, rows, fetched, j0, blocks, tp, bank_no):
+            bank = psum.tile([P, blocks, 2 * P], F32, name=tag, tag="bank%d" % bank_no)
+            for tt in range(2):
+                t = 2 * tp + tt
+                for jb in range(blocks):
+                    dst = bank[:, jb, tt * P : (tt + 1) * P]
+                    c0 = j0 + jb * P
+                    nc.tensor.matmul(dst, fetched[tt][:, jb * P : (jb + 1) * P], ident[:], start=True, stop=False, is_transpose=True)
+                    nc.tensor.matmul(dst, rows[t][:, c0 : c0 + P], ident[:], start=False, stop=True, is_transpose=True)
+            return bank[:]
+
+        h_banks = []
+        y_all = keep.tile([P, TILES, H], F32, name="yg", tag="yg", align_bytes=64)
+        w1_q = None
+        j0 = 0
+        for hb, width in enumerate(SPLIT):
+            blocks = width // P
+            z_turned = keep.tile([P, blocks, S], BF16, name="z_turned%d" % hb, align_bytes=64)
+            for tp in range(2):
+                d_fetched, y_fetched = [], []
+                for tt in range(2):
+                    t = 2 * tp + tt
+                    dg = ring.tile([P, width], F32, name="dg", tag="dg", bufs=8)
+                    gather(N2[hb][t], dg[:], ds[t], part(l2, j0, j0 + width))
+                    d_fetched.append(dg)
+                    yg = y_all[:, t, j0 : j0 + width]
+                    gather("s", yg, ys[t], part(l1, j0, j0 + width))
+                    y_fetched.append(yg)
+                d_sum = turned_sum("d_sum", ds, d_fetched, j0, blocks, tp, [4,5,6,7][2 * hb + tp])
+                y_sum = turned_sum("y_sum", ys, y_fetched, j0, blocks, tp, [0,1,2,3][2 * hb + tp])
+                th = keep.tile([P, blocks, 2 * P], F32, name="th%d" % (2 * hb + tp), align_bytes=64)
+                nc.scalar.activation(th[:], d_sum, ACT.Tanh, scale=0.5)
+                nc.vector.scalar_tensor_tensor(
+                    out=z_turned[:, :, tp * 2 * P : (tp + 1) * 2 * P],
+                    in0=th[:],
+                    scalar=1.0,
+                    in1=y_sum,
+                    op0=ALU.add,
+                    op1=ALU.mult,
+                )
+            if w1_q is None:
+                w1_q = quantise_weight("w1", w1_raw)
+            z_bank = psum.tile([P, 2, blocks, P], F32, name="z_bank", tag="bank%d" % [0,1][hb])
+            z_words = z_turned[:].rearrange("f jb c -> f (jb c)").bitcast(F32)
+            for jb in range(blocks):
+                for u in range(2):
+                    w0 = jb * 2 * P
+                    nc.tensor.transpose(z_bank[:, u, jb, :], z_words[:, w0 + u : w0 + 2 * P : 2], ident[:])
+            z_grouped = ring.tile([P, width * PACK], BF16, name="z_grouped", align_bytes=64)
+            copy(
+                ZCOPY[hb],
+                z_grouped[:].bitcast(F32).rearrange("p (c u) -> p c u", u=2),
+                z_bank[:].rearrange("p u jb f -> p (jb f) u"),
+            )
+            z_codes = ring.tile([P, width], U32, name="z_codes", align_bytes=64)
+            z_scales = ring.tile([P, width], U8, name="z_scales", align_bytes=64)
+            nc.vector.quantize_mx(out=z_codes[:].bitcast(FP8X4), scales=z_scales[:], in_=z_grouped[:])
+            for mp in range(2):
+                bank = psum.tile([P, 2, width], F32, name="hmm", tag="bank%d" % [[4,5],[6,7]][hb][mp])
+                for mm in range(2):
+                    mt = 2 * mp + mm
+                    mx(bank[:, mm, :], w1_q, slice(mt * P, (mt + 1) * P), (z_codes, z_scales), slice(0, width))
+                    h_banks.append((hb, mt, j0, width, bank[:, mm, :]))
+            j0 = j0 + width
+
+        hs = [keep.tile([P, H], F32, name="h%d" % mt, tag=TAGS.get("h%d" % mt, "h%d" % mt), align_bytes=64) for mt in range(TILES)]
+        for hb, mt, j0, width, src in h_banks:
+            copy(HCOPY[hb][mt], hs[mt][:, j0 : j0 + width], src)
+
+        for mt in range(2, TILES):
+            fetch("4", tab4, "s", l4, mt)
+            fetch("3", tab3, N3[mt], l3, mt)
+
+        for mt in range(TILES):
+            res = keep.tile([P, H], F32, name="res%d" % mt)
+            for hb in range(2):
+                hg = ring.tile([P, HALF], F32, name="hg", tag="hg", bufs=4)
+                gather("s", hg[:], hs[mt], part(l5, hb * HALF, (hb + 1) * HALF))
+                prod = ring.tile([P, HALF], F32, name="prod", tag="prod", bufs=4)
+                nc.vector.tensor_tensor(prod[:], hg[:], tab3[mt][:, hb * HALF : (hb + 1) * HALF], ALU.mult)
+                nc.vector.tensor_tensor(res[:, hb * HALF : (hb + 1) * HALF], prod[:], tab4[mt][:, hb * HALF : (hb + 1) * HALF], ALU.add)
+            nc.sync.dma_start(out=out[mt * P : (mt + 1) * P, :], in_=res[:])

@@ -21,25 +21,27 @@ PACK = 4
 TILES = 4
 HALF = 256
 LIST_ROWS = 16
+TAGS = {"tab4_3":"d3","tab3_3":"y3","tab3_2":"z_turned","w1_bf16":"th2_0"}
+HCOPY = "svvv"
+ZCOPY = "vs"
 YCOPY = "ssss"
 DCOPY = "vvvv"
-N2 = ["vvvv","vvss"]
-N3 = "vvvs"
-ZCOPY = "vv"
-HCOPY = ["ssss","vvvv"]
-CAST = {"wa":"v","wb":"s","w1":"v"}
-SPLIT = [256,256]
-LATE = [2,3]
-TAGS = {"wb_codes":"x_codes","tab4_3":"d3","tab3_2":"wb_bf16","tab3_3":"yg","h0":"y0","h1":"y1","h2":"y2","h3":"y3"}
-HOLD = 0
+N2 = "vvvvvvvv"
+N3 = "vvss"
+WIDE = [0,0,0,0]
+WB_SCALAR = 384
+XSPLIT = 2
 
 
 def tile_picked_twttriebkinda_none_p_kernel(tc, x_words, x_scales, wa, wb, gt, w1, tab, offs, two, n1, n2, n3, n4, n5, out):
     nc = tc.nc
     with ExitStack() as ctx:
         keep = ctx.enter_context(tc.tile_pool(name="keep", bufs=1))
-        ring = ctx.enter_context(tc.tile_pool(name="ring", bufs=2))
+        ring = ctx.enter_context(tc.tile_pool(name="ring", bufs=4))
         psum = ctx.enter_context(tc.psum_pool(name="psum", bufs=1))
+
+        def held(name, shape, dtype):
+            return keep.tile(shape, dtype, name=name, tag=TAGS.get(name, name), align_bytes=64)
 
         def load_list(name, src):
             tile = keep.tile([P, S // LIST_ROWS], U16, name=name)
@@ -47,23 +49,26 @@ def tile_picked_twttriebkinda_none_p_kernel(tc, x_words, x_scales, wa, wb, gt, w
             return tile
 
         def load_weight(name, src):
-            raw = keep.tile([P, PACK, 512], F32, name=name)
+            raw = held(name, [P, PACK, 512], F32)
             nc.sync.dma_start(out=raw[:], in_=src.rearrange("(p j) n -> p j n", j=PACK))
             return raw
 
         def load_tab(mt):
-            tile = keep.tile([P, J], F32, name="tab%d" % mt)
+            tile = held("tab%d" % mt, [P, J], F32)
             nc.sync.dma_start(out=tile[:], in_=tab[mt * P : (mt + 1) * P, :])
             return tile
 
         def part(lst, c0, c1):
             return lst[:, c0 // LIST_ROWS : c1 // LIST_ROWS]
 
-        def gather(eng, dst, window, lst):
+        def half(hb):
+            return slice(hb * HALF, (hb + 1) * HALF)
+
+        def gather(eng, dst, window, lst, hb):
             if eng == "s":
-                nc.scalar.activation(dst, window[:].indirect(lst), ACT.Copy)
+                nc.scalar.activation(dst, window[:].indirect(part(lst, hb * HALF, (hb + 1) * HALF)), ACT.Copy)
             else:
-                nc.vector.tensor_copy(dst, window[:].indirect(lst))
+                nc.vector.tensor_copy(dst, window[:].indirect(part(lst, hb * HALF, (hb + 1) * HALF)))
 
         def copy(eng, dst, src):
             if eng == "s":
@@ -73,10 +78,12 @@ def tile_picked_twttriebkinda_none_p_kernel(tc, x_words, x_scales, wa, wb, gt, w
             else:
                 nc.gpsimd.tensor_copy(dst, src)
 
-        x_bytes = keep.tile([P, T], U8, name="x_bytes", align_bytes=64)
+        x_bytes = held("x_bytes", [P, T], U8)
         nc.vector.memset(x_bytes[:].bitcast(I32), 0)
-        x_codes = keep.tile([P, T], U32, name="x_codes", align_bytes=64)
+        x_codes = held("x_codes", [P, T], U32)
         gt_cols = keep.tile([P, TILES], F32, name="gt_cols")
+        with nc.allow_non_contiguous_dma(reason="one weight a row"):
+            nc.scalar.dma_start(out=gt_cols[:], in_=gt.rearrange("(t p) o -> p (t o)", p=P))
         tabs = [None] * TILES
         l4 = load_list("l4", n4)
         tabs[0] = load_tab(0)
@@ -98,8 +105,6 @@ def tile_picked_twttriebkinda_none_p_kernel(tc, x_words, x_scales, wa, wb, gt, w
         w1_raw = load_weight("w1_raw", w1)
         tabs[3] = load_tab(3)
         l5 = load_list("l5", n5)
-        with nc.allow_non_contiguous_dma(reason="one weight a row"):
-            nc.scalar.dma_start(out=gt_cols[:], in_=gt.rearrange("(t p) o -> p (t o)", p=P))
 
         ident = keep.tile([P, P], F32, name="ident")
         make_identity(nc, ident[:])
@@ -109,35 +114,34 @@ def tile_picked_twttriebkinda_none_p_kernel(tc, x_words, x_scales, wa, wb, gt, w
         tab3, tab4 = {}, {}
 
         def fetch(key, store, eng, lst, mt):
-            name = "tab%s_%d" % (key, mt)
-            tile = keep.tile([P, H], F32, name=name, tag=TAGS.get(name, name), align_bytes=64)
+            tile = held("tab%s_%d" % (key, mt), [P, H], F32)
             for hb in range(2):
-                gather(eng, tile[:, hb * HALF : (hb + 1) * HALF], tabs[mt], part(lst, hb * HALF, (hb + 1) * HALF))
+                gather(eng, tile[:, half(hb)], tabs[mt], lst, hb)
             store[mt] = tile
 
         for mt in range(2):
             fetch("4", tab4, "s", l4, mt)
             fetch("3", tab3, N3[mt], l3, mt)
 
-        def pick(name, dtype, window, lst):
-            picked = keep.tile([P, S], dtype, name=name, align_bytes=64)
-            nc.vector.tensor_copy(picked[:], window[:].indirect(lst[:]))
-            return picked
-
-        def quantise_weight(name, raw):
-            grouped = keep.tile([P, 512, PACK], BF16, name=name + "_bf16", tag=TAGS.get(name + "_bf16", name + "_bf16"), align_bytes=64)
-            engs = CAST[name]
-            width = 512 // len(engs)
-            for k, eng in enumerate(engs):
+        def round_weight(name, raw, shares):
+            grouped = held(name + "_bf16", [P, 512, PACK], BF16)
+            for eng, c0, c1 in shares:
+                i = 1 if eng == "g" else 4
                 copy(
                     eng,
-                    grouped[:, k * width : (k + 1) * width, :].rearrange("p (c i) j -> p c j i", i=4),
-                    raw[:, :, k * width : (k + 1) * width].rearrange("p j (c i) -> p c j i", i=4),
+                    grouped[:, c0:c1, :].rearrange("p (c i) j -> p c j i", i=i),
+                    raw[:, :, c0:c1].rearrange("p j (c i) -> p c j i", i=i),
                 )
-            codes = keep.tile([P, 512], U32, name=name + "_codes", tag=TAGS.get(name + "_codes", name + "_codes"), align_bytes=64)
-            scales = keep.tile([P, 512], U8, name=name + "_scales", align_bytes=64)
-            nc.vector.quantize_mx(out=codes[:].bitcast(FP8X4), scales=scales[:], in_=grouped[:].rearrange("p c j -> p (c j)"))
+            return grouped
+
+        def quantise(name, values, width):
+            codes = held(name + "_codes", [P, width], U32)
+            scales = held(name + "_scales", [P, width], U8)
+            nc.vector.quantize_mx(out=codes[:].bitcast(FP8X4), scales=scales[:], in_=values)
             return codes, scales
+
+        def quantise_weight(name, raw, shares):
+            return quantise(name, round_weight(name, raw, shares)[:].rearrange("p c j -> p (c j)"), 512)
 
         def mx(acc, lhs, lhs_cols, rhs, rhs_cols):
             nc.tensor.matmul_mx(
@@ -150,115 +154,111 @@ def tile_picked_twttriebkinda_none_p_kernel(tc, x_words, x_scales, wa, wb, gt, w
                 stop=True,
             )
 
-        ys, ds = [], []
+        wa_q = quantise_weight("wa", wa_raw, [("v", 0, 512)])
+        x_offs = (held("offs_codes", [P, S], U32), held("offs_scales", [P, S], U8))
+        x_two = (held("two_codes", [P, S], U32), held("two_scales", [P, S], U8))
+        nc.vector.tensor_copy(x_offs[1][:], x_bytes[:].indirect(l_offs[:]))
+        nc.vector.tensor_copy(x_two[1][:], x_bytes[:].indirect(l_two[:]))
+        wb_q = quantise_weight("wb", wb_raw, [("s", 0, WB_SCALAR), ("v", WB_SCALAR, 512)])
+        for k in range(XSPLIT):
+            c0, c1 = k * S // XSPLIT, (k + 1) * S // XSPLIT
+            for picked, lst in ((x_offs, l_offs), (x_two, l_two)):
+                nc.vector.tensor_copy(picked[0][:, c0:c1], x_codes[:].indirect(part(lst, c0, c1)))
+        fetch("4", tab4, "s", l4, 2)
 
-        def project_y(x_offs, wa_q):
-            for t in range(TILES):
-                bank = psum.tile([P, H], F32, name="ymm", tag="bank%d" % t)
-                mx(bank[:], x_offs, slice(t * P, (t + 1) * P), wa_q, slice(0, H))
-                y = keep.tile([P, H], F32, name="y%d" % t, align_bytes=64)
-                if YCOPY[t] == "s":
-                    nc.scalar.activation(y[:], bank[:], ACT.Copy, scale=half_gt[:, t : t + 1])
-                else:
-                    nc.vector.tensor_scalar(y[:], bank[:], half_gt[:, t : t + 1], None, ALU.mult)
-                ys.append(y)
+        def turned_sum(tag, rows, fetched, jb0, blocks):
+            bank = psum.tile([P, blocks, P], F32, name=tag, tag=tag, bufs=3)
+            for jj in range(blocks):
+                cols = slice((jb0 + jj) * P, (jb0 + jj + 1) * P)
+                nc.tensor.matmul(bank[:, jj, :], fetched[:, cols], ident[:], start=True, stop=False, is_transpose=True)
+                nc.tensor.matmul(bank[:, jj, :], rows[:, cols], ident[:], start=False, stop=True, is_transpose=True)
+            return bank
 
-        def project_d(x_two, wb_q):
-            for t in range(TILES):
-                bank = psum.tile([P, H], F32, name="dmm", tag="bank%d" % (4 + t))
-                mx(bank[:], x_two, slice(t * P, (t + 1) * P), wb_q, slice(0, H))
-                d = keep.tile([P, H], F32, name="d%d" % t, align_bytes=64)
-                copy(DCOPY[t], d[:], bank[:])
-                ds.append(d)
+        def by_pairs(bank):
+            return bank[:].rearrange("f jb (q u e) -> f u (jb q) e", u=2, e=2)
 
-        offs_scales = pick("offs_scales", U8, x_bytes, l_offs)
-        two_scales = pick("two_scales", U8, x_bytes, l_two)
-        wa_q = quantise_weight("wa", wa_raw)
-        offs_codes = pick("offs_codes", U32, x_codes, l_offs)
-        two_codes = pick("two_codes", U32, x_codes, l_two)
-        wb_q = quantise_weight("wb", wb_raw)
-        project_y((offs_codes, offs_scales), wa_q)
-        project_d((two_codes, two_scales), wb_q)
-
-        def turned_sum(tag, rows, fetched, j0, blocks, tp, bank_no):
-            bank = psum.tile([P, blocks, 2 * P], F32, name=tag, tag="bank%d" % bank_no)
-            for tt in range(2):
-                t = 2 * tp + tt
-                for jb in range(blocks):
-                    dst = bank[:, jb, tt * P : (tt + 1) * P]
-                    c0 = j0 + jb * P
-                    nc.tensor.matmul(dst, fetched[tt][:, jb * P : (jb + 1) * P], ident[:], start=True, stop=False, is_transpose=True)
-                    nc.tensor.matmul(dst, rows[t][:, c0 : c0 + P], ident[:], start=False, stop=True, is_transpose=True)
-            return bank[:]
-
-        h_banks = []
-        y_all = keep.tile([P, TILES, H], F32, name="yg", tag="yg", align_bytes=64)
-        w1_q = None
-        j0 = 0
-        for hb, width in enumerate(SPLIT):
-            blocks = width // P
-            z_turned = keep.tile([P, blocks, S], BF16, name="z_turned%d" % hb, align_bytes=64)
-            for tp in range(2):
-                d_fetched, y_fetched = [], []
-                for tt in range(2):
-                    t = 2 * tp + tt
-                    dg = ring.tile([P, width], F32, name="dg", tag="dg", bufs=8)
-                    gather(N2[hb][t], dg[:], ds[t], part(l2, j0, j0 + width))
-                    d_fetched.append(dg)
-                    yg = y_all[:, t, j0 : j0 + width]
-                    gather("s", yg, ys[t], part(l1, j0, j0 + width))
-                    y_fetched.append(yg)
-                d_sum = turned_sum("d_sum", ds, d_fetched, j0, blocks, tp, [4,5,6,7][2 * hb + tp])
-                y_sum = turned_sum("y_sum", ys, y_fetched, j0, blocks, tp, [0,1,2,3][2 * hb + tp])
-                th = keep.tile([P, blocks, 2 * P], F32, name="th%d" % (2 * hb + tp), align_bytes=64)
-                nc.scalar.activation(th[:], d_sum, ACT.Tanh, scale=0.5)
+        z_turned = held("z_turned", [P, 2, TILES, HALF], BF16)
+        def gate(t, y, yg, d, dg, jb0, blocks):
+            y_sum = turned_sum("y_sum", y, yg, jb0, blocks)
+            d_sum = turned_sum("d_sum", d, dg, jb0, blocks)
+            th = held("th%d_%d" % (t, jb0 // 2), [P, 2, blocks * 32, 2], F32)
+            nc.scalar.activation(th[:], by_pairs(d_sum), ACT.Tanh, scale=0.5)
+            for u in range(2):
                 nc.vector.scalar_tensor_tensor(
-                    out=z_turned[:, :, tp * 2 * P : (tp + 1) * 2 * P],
-                    in0=th[:],
+                    out=z_turned[:, u, jb0 : jb0 + blocks, t * 64 : (t + 1) * 64],
+                    in0=th[:, u],
                     scalar=1.0,
-                    in1=y_sum,
+                    in1=by_pairs(y_sum)[:, u],
                     op0=ALU.add,
                     op1=ALU.mult,
                 )
-            if w1_q is None:
-                w1_q = quantise_weight("w1", w1_raw)
-            z_bank = psum.tile([P, 2, blocks, P], F32, name="z_bank", tag="bank%d" % [0,1][hb])
-            z_words = z_turned[:].rearrange("f jb c -> f (jb c)").bitcast(F32)
-            for jb in range(blocks):
+
+        def project(t):
+            rows = slice(t * P, (t + 1) * P)
+            y_bank = psum.tile([P, H], F32, name="ymm", tag="ymm", bufs=1)
+            mx(y_bank[:], x_offs, rows, wa_q, slice(0, H))
+            d_bank = psum.tile([P, H], F32, name="dmm", tag="dmm", bufs=1)
+            mx(d_bank[:], x_two, rows, wb_q, slice(0, H))
+            return y_bank, d_bank
+
+        ahead = project(0)
+        for t in range(TILES):
+            y_bank, d_bank = ahead
+            y = held("y%d" % t, [P, H], F32)
+            if YCOPY[t] == "s":
+                nc.scalar.activation(y[:], y_bank[:], ACT.Copy, scale=half_gt[:, t : t + 1])
+            else:
+                nc.vector.tensor_scalar(y[:], y_bank[:], half_gt[:, t : t + 1], None, ALU.mult)
+            d = held("d%d" % t, [P, H], F32)
+            copy(DCOPY[t], d[:], d_bank[:])
+            if t + 1 < TILES:
+                ahead = project(t + 1)
+            yg = ring.tile([P, H], F32, name="yg", bufs=2)
+            dg = ring.tile([P, H], F32, name="dg", bufs=2)
+            for hb in range(2):
+                gather("s", yg[:, half(hb)], y, l1, hb)
+                gather(N2[2 * t + hb], dg[:, half(hb)], d, l2, hb)
+                if t in [3]:
+                    gate(t, y, yg, d, dg, 2 * hb, 2)
+            if t not in [3]:
+                gate(t, y, yg, d, dg, 0, TILES)
+
+        w1_q = quantise_weight("w1", w1_raw, [("v", 0, 512)])
+        z_words = z_turned[:].rearrange("f u jb c -> f (u jb c)").bitcast(F32)
+        z_q = []
+        for hb in range(2):
+            z_bank = psum.tile([P, 2, 2, P], F32, name="z_bank", tag=("ymm", "dmm")[hb], bufs=1)
+            for jj in range(2):
                 for u in range(2):
-                    w0 = jb * 2 * P
-                    nc.tensor.transpose(z_bank[:, u, jb, :], z_words[:, w0 + u : w0 + 2 * P : 2], ident[:])
-            z_grouped = ring.tile([P, width * PACK], BF16, name="z_grouped", align_bytes=64)
+                    w0 = (u * TILES + 2 * hb + jj) * P
+                    nc.tensor.transpose(z_bank[:, u, jj, :], z_words[:, w0 : w0 + P], ident[:])
+            z_grouped = held("z_grouped%d" % hb, [P, HALF * PACK], BF16)
             copy(
                 ZCOPY[hb],
                 z_grouped[:].bitcast(F32).rearrange("p (c u) -> p c u", u=2),
                 z_bank[:].rearrange("p u jb f -> p (jb f) u"),
             )
-            z_codes = ring.tile([P, width], U32, name="z_codes", align_bytes=64)
-            z_scales = ring.tile([P, width], U8, name="z_scales", align_bytes=64)
-            nc.vector.quantize_mx(out=z_codes[:].bitcast(FP8X4), scales=z_scales[:], in_=z_grouped[:])
-            for mp in range(2):
-                bank = psum.tile([P, 2, width], F32, name="hmm", tag="bank%d" % [[4,5],[6,7]][hb][mp])
-                for mm in range(2):
-                    mt = 2 * mp + mm
-                    mx(bank[:, mm, :], w1_q, slice(mt * P, (mt + 1) * P), (z_codes, z_scales), slice(0, width))
-                    h_banks.append((hb, mt, j0, width, bank[:, mm, :]))
-            j0 = j0 + width
+            z_q.append(quantise("z%d" % hb, z_grouped[:], HALF))
+        hs = [held("h%d" % mt, [P, H], F32) for mt in range(TILES)]
+        for mt in range(TILES):
+            for hb in range(2):
+                tag, bufs = [["ymm",1],["dmm",1],["d_sum",3],["y_sum",3],["d_sum",3],["y_sum",3],["d_sum",3],["y_sum",3]][2 * mt + hb]
+                h_bank = psum.tile([P, HALF], F32, name="hmm", tag=tag, bufs=bufs)
+                mx(h_bank[:], w1_q, slice(mt * P, (mt + 1) * P), z_q[hb], slice(0, HALF))
+                copy("vsvsvvvv"[2 * mt + hb], hs[mt][:, half(hb)], h_bank[:])
 
-        hs = [keep.tile([P, H], F32, name="h%d" % mt, tag=TAGS.get("h%d" % mt, "h%d" % mt), align_bytes=64) for mt in range(TILES)]
-        for hb, mt, j0, width, src in h_banks:
-            copy(HCOPY[hb][mt], hs[mt][:, j0 : j0 + width], src)
-
-        for mt in range(2, TILES):
-            fetch("4", tab4, "s", l4, mt)
-            fetch("3", tab3, N3[mt], l3, mt)
+        fetch("4", tab4, "s", l4, 3)
+        fetch("3", tab3, N3[3], l3, 3)
+        fetch("3", tab3, N3[2], l3, 2)
 
         for mt in range(TILES):
-            res = keep.tile([P, H], F32, name="res%d" % mt)
+            res = held("res%d" % mt, [P, H], F32)
+            hg = ring.tile([P, H], F32, name="hg", bufs=2)
+            prod = ring.tile([P, H], F32, name="prod", bufs=2)
             for hb in range(2):
-                hg = ring.tile([P, HALF], F32, name="hg", tag="hg", bufs=4)
-                gather("s", hg[:], hs[mt], part(l5, hb * HALF, (hb + 1) * HALF))
-                prod = ring.tile([P, HALF], F32, name="prod", tag="prod", bufs=4)
-                nc.vector.tensor_tensor(prod[:], hg[:], tab3[mt][:, hb * HALF : (hb + 1) * HALF], ALU.mult)
-                nc.vector.tensor_tensor(res[:, hb * HALF : (hb + 1) * HALF], prod[:], tab4[mt][:, hb * HALF : (hb + 1) * HALF], ALU.add)
-            nc.sync.dma_start(out=out[mt * P : (mt + 1) * P, :], in_=res[:])
+                gather("s", hg[:, half(hb)], hs[mt], l5, hb)
+            for cols in ([slice(0, H)] if WIDE[mt] else [half(0), half(1)]):
+                nc.vector.tensor_tensor(prod[:, cols], hg[:, cols], tab3[mt][:, cols], ALU.mult)
+                nc.vector.tensor_tensor(res[:, cols], prod[:, cols], tab4[mt][:, cols], ALU.add)
+            for cols in ([slice(0, H)] if mt < TILES - 1 else [half(0), half(1)]):
+                nc.sync.dma_start(out=out[mt * P : (mt + 1) * P, cols], in_=res[:, cols])

@@ -27,9 +27,9 @@ ZCOPY = "vs"
 YCOPY = "ssss"
 DCOPY = "vvvv"
 N2 = "vvvvvvvv"
-N3 = "vvss"
+N3 = "vsss"
 WIDE = [0,0,0,0]
-WB_SCALAR = 384
+WB_SCALAR = 256
 XSPLIT = 2
 
 
@@ -81,23 +81,23 @@ def tile_picked_twttriebkinda_none_p_kernel(tc, x_words, x_scales, wa, wb, gt, w
         x_bytes = held("x_bytes", [P, T], U8)
         nc.vector.memset(x_bytes[:].bitcast(I32), 0)
         x_codes = held("x_codes", [P, T], U32)
-        gt_cols = keep.tile([P, TILES], F32, name="gt_cols")
-        with nc.allow_non_contiguous_dma(reason="one weight a row"):
-            nc.scalar.dma_start(out=gt_cols[:], in_=gt.rearrange("(t p) o -> p (t o)", p=P))
+        gt_rows = keep.tile([P, P], F32, name="gt_rows")
+        nc.vector.memset(gt_rows[:], 0.0)
         tabs = [None] * TILES
         l4 = load_list("l4", n4)
         tabs[0] = load_tab(0)
         l3 = load_list("l3", n3)
-        tabs[1] = load_tab(1)
-        l_offs = load_list("l_offs", offs)
-        l_two = load_list("l_two", two)
-        wa_raw = load_weight("wa_raw", wa)
         for q in range(4):
             nc.sync.dma_start(
                 out=x_bytes[32 * q : 32 * q + 4, :].bitcast(I32),
                 in_=x_scales[0, 4 * q : 4 * q + 4, :].bitcast(I32),
             )
+        wa_raw = load_weight("wa_raw", wa)
+        l_offs = load_list("l_offs", offs)
+        l_two = load_list("l_two", two)
+        tabs[1] = load_tab(1)
         wb_raw = load_weight("wb_raw", wb)
+        nc.sync.dma_start(out=gt_rows[0:TILES, :], in_=gt.rearrange("(t p) o -> t (p o)", p=P))
         nc.sync.dma_start(out=x_codes[:].bitcast(I32), in_=x_words[0].rearrange("p n t -> p (n t)").bitcast(I32))
         tabs[2] = load_tab(2)
         l1 = load_list("l1", n1)
@@ -109,7 +109,9 @@ def tile_picked_twttriebkinda_none_p_kernel(tc, x_words, x_scales, wa, wb, gt, w
         ident = keep.tile([P, P], F32, name="ident")
         make_identity(nc, ident[:])
         half_gt = keep.tile([P, TILES], F32, name="half_gt")
-        nc.vector.tensor_scalar(half_gt[:], gt_cols[:], 0.5, None, ALU.mult)
+        gt_bank = psum.tile([P, P], F32, name="gt_bank", tag="y_sum", bufs=3)
+        nc.tensor.transpose(gt_bank[:], gt_rows[:], ident[:])
+        nc.scalar.activation(half_gt[:], gt_bank[:, 0:TILES], ACT.Copy, scale=0.5)
 
         tab3, tab4 = {}, {}
 
@@ -167,7 +169,7 @@ def tile_picked_twttriebkinda_none_p_kernel(tc, x_words, x_scales, wa, wb, gt, w
         fetch("4", tab4, "s", l4, 2)
 
         def turned_sum(tag, rows, fetched, jb0, blocks):
-            bank = psum.tile([P, blocks, P], F32, name=tag, tag=tag, bufs=3)
+            bank = psum.tile([P, blocks, P], F32, name=tag, tag=tag, bufs={"y_sum": 3, "d_sum": 3}[tag])
             for jj in range(blocks):
                 cols = slice((jb0 + jj) * P, (jb0 + jj + 1) * P)
                 nc.tensor.matmul(bank[:, jj, :], fetched[:, cols], ident[:], start=True, stop=False, is_transpose=True)
@@ -227,7 +229,7 @@ def tile_picked_twttriebkinda_none_p_kernel(tc, x_words, x_scales, wa, wb, gt, w
         z_words = z_turned[:].rearrange("f u jb c -> f (u jb c)").bitcast(F32)
         z_q = []
         for hb in range(2):
-            z_bank = psum.tile([P, 2, 2, P], F32, name="z_bank", tag=("ymm", "dmm")[hb], bufs=1)
+            z_bank = psum.tile([P, 2, 2, P], F32, name="z_bank", tag=("ymm", "dmm")[hb], bufs=(1, 1)[hb])
             for jj in range(2):
                 for u in range(2):
                     w0 = (u * TILES + 2 * hb + jj) * P
@@ -242,7 +244,7 @@ def tile_picked_twttriebkinda_none_p_kernel(tc, x_words, x_scales, wa, wb, gt, w
         hs = [held("h%d" % mt, [P, H], F32) for mt in range(TILES)]
         for mt in range(TILES):
             for hb in range(2):
-                tag, bufs = [["ymm",1],["dmm",1],["d_sum",3],["y_sum",3],["d_sum",3],["y_sum",3],["d_sum",3],["y_sum",3]][2 * mt + hb]
+                tag, bufs = [["ymm",1],["d_sum",3],["dmm",1],["y_sum",3],["ymm",1],["d_sum",3],["dmm",1],["y_sum",3]][2 * mt + hb]
                 h_bank = psum.tile([P, HALF], F32, name="hmm", tag=tag, bufs=bufs)
                 mx(h_bank[:], w1_q, slice(mt * P, (mt + 1) * P), z_q[hb], slice(0, HALF))
                 copy("vsvsvvvv"[2 * mt + hb], hs[mt][:, half(hb)], h_bank[:])
@@ -255,10 +257,14 @@ def tile_picked_twttriebkinda_none_p_kernel(tc, x_words, x_scales, wa, wb, gt, w
             res = held("res%d" % mt, [P, H], F32)
             hg = ring.tile([P, H], F32, name="hg", bufs=2)
             prod = ring.tile([P, H], F32, name="prod", bufs=2)
-            for hb in range(2):
-                gather("s", hg[:, half(hb)], hs[mt], l5, hb)
-            for cols in ([slice(0, H)] if WIDE[mt] else [half(0), half(1)]):
+            c0 = 0
+            for width in ([HALF, HALF] if mt < TILES - 1 else [256,256]):
+                cols = slice(c0, c0 + width)
+                nc.scalar.activation(hg[:, cols], hs[mt][:].indirect(part(l5, c0, c0 + width)), ACT.Copy)
                 nc.vector.tensor_tensor(prod[:, cols], hg[:, cols], tab3[mt][:, cols], ALU.mult)
                 nc.vector.tensor_tensor(res[:, cols], prod[:, cols], tab4[mt][:, cols], ALU.add)
-            for cols in ([slice(0, H)] if mt < TILES - 1 else [half(0), half(1)]):
-                nc.sync.dma_start(out=out[mt * P : (mt + 1) * P, cols], in_=res[:, cols])
+                if mt == TILES - 1:
+                    nc.sync.dma_start(out=out[mt * P : (mt + 1) * P, cols], in_=res[:, cols])
+                c0 = c0 + width
+            if mt < TILES - 1:
+                nc.sync.dma_start(out=out[mt * P : (mt + 1) * P, :], in_=res[:])

from contextlib import ExitStack

import concourse.mybir as mybir
from concourse.masks import make_identity

K, T, S, N, H, J = 512, 2048, 512, 512, 512, 512
FLOPS = 2 * S * K * H * 2 + 2 * N * S * H

F32 = mybir.dt.float32
BF16 = mybir.dt.bfloat16
I32 = mybir.dt.int32
U32 = mybir.dt.uint32
U16 = mybir.dt.uint16
U8 = mybir.dt.uint8
FP8X4 = mybir.dt.float8_e4m3fn_x4
ACT = mybir.ActivationFunctionType
ALU = mybir.AluOpType

P = 128
PACK = 4
TILES = 4
HALF = 256
LIST_ROWS = 16
TAGS = {"tab4_3":"d3","tab3_3":"y3","tab3_2":"z_turned","w1_bf16":"th2_0"}
HCOPY = "svvv"
ZCOPY = "vs"
YCOPY = "ssss"
DCOPY = "vvvv"
N2 = "vvvvvvvv"
N3 = "vsss"
WIDE = [0,0,0,0]
WB_SCALAR = 256
XSPLIT = 2


def tile_picked_twttriebkinda_none_p_kernel(tc, x_words, x_scales, wa, wb, gt, w1, tab, offs, two, n1, n2, n3, n4, n5, out):
    nc = tc.nc
    with ExitStack() as ctx:
        keep = ctx.enter_context(tc.tile_pool(name="keep", bufs=1))
        ring = ctx.enter_context(tc.tile_pool(name="ring", bufs=4))
        psum = ctx.enter_context(tc.psum_pool(name="psum", bufs=1))

        def held(name, shape, dtype):
            return keep.tile(shape, dtype, name=name, tag=TAGS.get(name, name), align_bytes=64)

        def load_list(name, src):
            tile = keep.tile([P, S // LIST_ROWS], U16, name=name)
            nc.sync.dma_start(tile[:], src)
            return tile

        def load_weight(name, src):
            raw = held(name, [P, PACK, 512], F32)
            nc.sync.dma_start(out=raw[:], in_=src.rearrange("(p j) n -> p j n", j=PACK))
            return raw

        def load_tab(mt):
            tile = held("tab%d" % mt, [P, J], F32)
            nc.sync.dma_start(out=tile[:], in_=tab[mt * P : (mt + 1) * P, :])
            return tile

        def part(lst, c0, c1):
            return lst[:, c0 // LIST_ROWS : c1 // LIST_ROWS]

        def half(hb):
            return slice(hb * HALF, (hb + 1) * HALF)

        def gather(eng, dst, window, lst, hb):
            if eng == "s":
                nc.scalar.activation(dst, window[:].indirect(part(lst, hb * HALF, (hb + 1) * HALF)), ACT.Copy)
            else:
                nc.vector.tensor_copy(dst, window[:].indirect(part(lst, hb * HALF, (hb + 1) * HALF)))

        def copy(eng, dst, src):
            if eng == "s":
                nc.scalar.copy(dst, src)
            elif eng == "v":
                nc.vector.tensor_copy(dst, src)
            else:
                nc.gpsimd.tensor_copy(dst, src)

        x_bytes = held("x_bytes", [P, T], U8)
        nc.vector.memset(x_bytes[:].bitcast(I32), 0)
        x_codes = held("x_codes", [P, T], U32)
        gt_rows = keep.tile([P, P], F32, name="gt_rows")
        nc.vector.memset(gt_rows[:], 0.0)
        tabs = [None] * TILES
        l4 = load_list("l4", n4)
        tabs[0] = load_tab(0)
        l3 = load_list("l3", n3)
        for q in range(4):
            nc.sync.dma_start(
                out=x_bytes[32 * q : 32 * q + 4, :].bitcast(I32),
                in_=x_scales[0, 4 * q : 4 * q + 4, :].bitcast(I32),
            )
        wa_raw = load_weight("wa_raw", wa)
        l_offs = load_list("l_offs", offs)
        l_two = load_list("l_two", two)
        tabs[1] = load_tab(1)
        wb_raw = load_weight("wb_raw", wb)
        nc.sync.dma_start(out=gt_rows[0:TILES, :], in_=gt.rearrange("(t p) o -> t (p o)", p=P))
        nc.sync.dma_start(out=x_codes[:].bitcast(I32), in_=x_words[0].rearrange("p n t -> p (n t)").bitcast(I32))
        tabs[2] = load_tab(2)
        l1 = load_list("l1", n1)
        l2 = load_list("l2", n2)
        w1_raw = load_weight("w1_raw", w1)
        tabs[3] = load_tab(3)
        l5 = load_list("l5", n5)

        ident = keep.tile([P, P], F32, name="ident")
        make_identity(nc, ident[:])
        half_gt = keep.tile([P, TILES], F32, name="half_gt")
        gt_bank = psum.tile([P, P], F32, name="gt_bank", tag="y_sum", bufs=3)
        nc.tensor.transpose(gt_bank[:], gt_rows[:], ident[:])
        nc.scalar.activation(half_gt[:], gt_bank[:, 0:TILES], ACT.Copy, scale=0.5)

        tab3, tab4 = {}, {}

        def fetch(key, store, eng, lst, mt):
            tile = held("tab%s_%d" % (key, mt), [P, H], F32)
            for hb in range(2):
                gather(eng, tile[:, half(hb)], tabs[mt], lst, hb)
            store[mt] = tile

        for mt in range(2):
            fetch("4", tab4, "s", l4, mt)
            fetch("3", tab3, N3[mt], l3, mt)

        def round_weight(name, raw, shares):
            grouped = held(name + "_bf16", [P, 512, PACK], BF16)
            for eng, c0, c1 in shares:
                i = 1 if eng == "g" else 4
                copy(
                    eng,
                    grouped[:, c0:c1, :].rearrange("p (c i) j -> p c j i", i=i),
                    raw[:, :, c0:c1].rearrange("p j (c i) -> p c j i", i=i),
                )
            return grouped

        def quantise(name, values, width):
            codes = held(name + "_codes", [P, width], U32)
            scales = held(name + "_scales", [P, width], U8)
            nc.vector.quantize_mx(out=codes[:].bitcast(FP8X4), scales=scales[:], in_=values)
            return codes, scales

        def quantise_weight(name, raw, shares):
            return quantise(name, round_weight(name, raw, shares)[:].rearrange("p c j -> p (c j)"), 512)

        def mx(acc, lhs, lhs_cols, rhs, rhs_cols):
            nc.tensor.matmul_mx(
                out=acc,
                lhsT=lhs[0][:, lhs_cols].bitcast(FP8X4),
                lhsT_scale=lhs[1][:, lhs_cols],
                rhs=rhs[0][:, rhs_cols].bitcast(FP8X4),
                rhs_scale=rhs[1][:, rhs_cols],
                start=True,
                stop=True,
            )

        wa_q = quantise_weight("wa", wa_raw, [("v", 0, 512)])
        x_offs = (held("offs_codes", [P, S], U32), held("offs_scales", [P, S], U8))
        x_two = (held("two_codes", [P, S], U32), held("two_scales", [P, S], U8))
        nc.vector.tensor_copy(x_offs[1][:], x_bytes[:].indirect(l_offs[:]))
        nc.vector.tensor_copy(x_two[1][:], x_bytes[:].indirect(l_two[:]))
        wb_q = quantise_weight("wb", wb_raw, [("s", 0, WB_SCALAR), ("v", WB_SCALAR, 512)])
        for k in range(XSPLIT):
            c0, c1 = k * S // XSPLIT, (k + 1) * S // XSPLIT
            for picked, lst in ((x_offs, l_offs), (x_two, l_two)):
                nc.vector.tensor_copy(picked[0][:, c0:c1], x_codes[:].indirect(part(lst, c0, c1)))
        fetch("4", tab4, "s", l4, 2)

        def turned_sum(tag, rows, fetched, jb0, blocks):
            bank = psum.tile([P, blocks, P], F32, name=tag, tag=tag, bufs={"y_sum": 3, "d_sum": 3}[tag])
            for jj in range(blocks):
                cols = slice((jb0 + jj) * P, (jb0 + jj + 1) * P)
                nc.tensor.matmul(bank[:, jj, :], fetched[:, cols], ident[:], start=True, stop=False, is_transpose=True)
                nc.tensor.matmul(bank[:, jj, :], rows[:, cols], ident[:], start=False, stop=True, is_transpose=True)
            return bank

        def by_pairs(bank):
            return bank[:].rearrange("f jb (q u e) -> f u (jb q) e", u=2, e=2)

        z_turned = held("z_turned", [P, 2, TILES, HALF], BF16)
        def gate(t, y, yg, d, dg, jb0, blocks):
            y_sum = turned_sum("y_sum", y, yg, jb0, blocks)
            d_sum = turned_sum("d_sum", d, dg, jb0, blocks)
            th = held("th%d_%d" % (t, jb0 // 2), [P, 2, blocks * 32, 2], F32)
            nc.scalar.activation(th[:], by_pairs(d_sum), ACT.Tanh, scale=0.5)
            for u in range(2):
                nc.vector.scalar_tensor_tensor(
                    out=z_turned[:, u, jb0 : jb0 + blocks, t * 64 : (t + 1) * 64],
                    in0=th[:, u],
                    scalar=1.0,
                    in1=by_pairs(y_sum)[:, u],
                    op0=ALU.add,
                    op1=ALU.mult,
                )

        def project(t):
            rows = slice(t * P, (t + 1) * P)
            y_bank = psum.tile([P, H], F32, name="ymm", tag="ymm", bufs=1)
            mx(y_bank[:], x_offs, rows, wa_q, slice(0, H))
            d_bank = psum.tile([P, H], F32, name="dmm", tag="dmm", bufs=1)
            mx(d_bank[:], x_two, rows, wb_q, slice(0, H))
            return y_bank, d_bank

        ahead = project(0)
        for t in range(TILES):
            y_bank, d_bank = ahead
            y = held("y%d" % t, [P, H], F32)
            if YCOPY[t] == "s":
                nc.scalar.activation(y[:], y_bank[:], ACT.Copy, scale=half_gt[:, t : t + 1])
            else:
                nc.vector.tensor_scalar(y[:], y_bank[:], half_gt[:, t : t + 1], None, ALU.mult)
            d = held("d%d" % t, [P, H], F32)
            copy(DCOPY[t], d[:], d_bank[:])
            if t + 1 < TILES:
                ahead = project(t + 1)
            yg = ring.tile([P, H], F32, name="yg", bufs=2)
            dg = ring.tile([P, H], F32, name="dg", bufs=2)
            for hb in range(2):
                gather("s", yg[:, half(hb)], y, l1, hb)
                gather(N2[2 * t + hb], dg[:, half(hb)], d, l2, hb)
                if t in [3]:
                    gate(t, y, yg, d, dg, 2 * hb, 2)
            if t not in [3]:
                gate(t, y, yg, d, dg, 0, TILES)

        w1_q = quantise_weight("w1", w1_raw, [("v", 0, 512)])
        z_words = z_turned[:].rearrange("f u jb c -> f (u jb c)").bitcast(F32)
        z_q = []
        for hb in range(2):
            z_bank = psum.tile([P, 2, 2, P], F32, name="z_bank", tag=("ymm", "dmm")[hb], bufs=(1, 1)[hb])
            for jj in range(2):
                for u in range(2):
                    w0 = (u * TILES + 2 * hb + jj) * P
                    nc.tensor.transpose(z_bank[:, u, jj, :], z_words[:, w0 : w0 + P], ident[:])
            z_grouped = held("z_grouped%d" % hb, [P, HALF * PACK], BF16)
            copy(
                ZCOPY[hb],
                z_grouped[:].bitcast(F32).rearrange("p (c u) -> p c u", u=2),
                z_bank[:].rearrange("p u jb f -> p (jb f) u"),
            )
            z_q.append(quantise("z%d" % hb, z_grouped[:], HALF))
        hs = [held("h%d" % mt, [P, H], F32) for mt in range(TILES)]
        for mt in range(TILES):
            for hb in range(2):
                tag, bufs = [["ymm",1],["d_sum",3],["dmm",1],["y_sum",3],["ymm",1],["d_sum",3],["dmm",1],["y_sum",3]][2 * mt + hb]
                h_bank = psum.tile([P, HALF], F32, name="hmm", tag=tag, bufs=bufs)
                mx(h_bank[:], w1_q, slice(mt * P, (mt + 1) * P), z_q[hb], slice(0, HALF))
                copy("vsvsvvvv"[2 * mt + hb], hs[mt][:, half(hb)], h_bank[:])

        fetch("4", tab4, "s", l4, 3)
        fetch("3", tab3, N3[3], l3, 3)
        fetch("3", tab3, N3[2], l3, 2)

        for mt in range(TILES):
            res = held("res%d" % mt, [P, H], F32)
            hg = ring.tile([P, H], F32, name="hg", bufs=2)
            prod = ring.tile([P, H], F32, name="prod", bufs=2)
            c0 = 0
            for width in ([HALF, HALF] if mt < TILES - 1 else [256,256]):
                cols = slice(c0, c0 + width)
                nc.scalar.activation(hg[:, cols], hs[mt][:].indirect(part(l5, c0, c0 + width)), ACT.Copy)
                nc.vector.tensor_tensor(prod[:, cols], hg[:, cols], tab3[mt][:, cols], ALU.mult)
                nc.vector.tensor_tensor(res[:, cols], prod[:, cols], tab4[mt][:, cols], ALU.add)
                if mt == TILES - 1:
                    nc.sync.dma_start(out=out[mt * P : (mt + 1) * P, cols], in_=res[:, cols])
                c0 = c0 + width
            if mt < TILES - 1:
                nc.sync.dma_start(out=out[mt * P : (mt + 1) * P, :], in_=res[:])
